import numpy as np, ml_dtypes
CORES = [40,64,80,88,96,104,120,144]
N = 8
BF = ml_dtypes.bfloat16
L, S, ST, GENS, K = 128, 9, 4, 2, 32
GW, XW = S * L, 16 * L
def parts(rng):
    g = rng.integers(0, XW, (N, 8, 16, GW)); h = rng.integers(0, GW, (N, 8, 16, GW)); x = rng.integers(0, 256, (N, 8, 16, XW))
    return g, h, x, rng.integers(0, 256, (N, 8, 16, L)), rng.integers(800, 1151, (N, 8))
def pack(g, h, x, a, t):
    return {"gn": np.ascontiguousarray(g.reshape(N, 128, GW)).astype(np.int32), "nb": np.ascontiguousarray(h.reshape(N, 128, GW)).astype(np.int32),
            "x": x.reshape(N, 128, XW).astype(np.float32).astype(BF), "th": np.repeat(t, 16, axis=1).reshape(N, 128, 1).astype(np.int32), "a0": a.reshape(N, 128, L).astype(np.float32).astype(BF)}
def setup_inputs(rng):
    return pack(*parts(rng))
def uneven(rng, n):
    v = np.floor(256 * rng.random((N, 8, 16, n)) * np.exp2(-rng.integers(0, 8, (N, 8, 1, n)).astype(np.float64))).astype(np.int64)
    return np.where(rng.random((N, 8, 1, n)) < 0.5, 255 - v, v)
def setup_inputs_spread(rng):
    g = (XW * rng.random((N, 8, 16, GW)) ** 3).astype(np.int64); h = (GW * rng.random((N, 8, 16, GW)) ** 2).astype(np.int64)
    g[:, 1::2] = XW - 1 - g[:, 1::2]; h[:, :, ::2] = GW - 1 - h[:, :, ::2]
    t = np.argsort(rng.random((N, 8)), axis=1) * 510 + rng.integers(0, 510, (N, 8))
    return pack(g, h, uneven(rng, XW), uneven(rng, L), t)
def twoends(rng, n):
    return np.where(rng.random((N, 8, 1, n)) < 0.7, 255 * rng.integers(0, 2, (N, 8, 1, n)), 255 * rng.integers(0, 2, (N, 8, 16, n)))
def setup_inputs_ends(rng):
    g, h, x, a, t = parts(rng)
    g = np.where(rng.random(g.shape) < 0.8, (XW - 1) * rng.integers(0, 2, g.shape), g); h = np.where(rng.random(h.shape) < 0.8, (GW - 1) * rng.integers(0, 2, h.shape), h)
    x = twoends(rng, XW); a = twoends(rng, L); x[..., 0] = 0; x[..., XW - 1] = 255
    for q in range(N): t[q, :7] = rng.permutation(np.array([0, 0, 4080, 4080, 4080, 2294, 2294]))
    t[:, 7] = 0
    for i in (0, 1, L - 2, L - 1):
        g[:, 7, 0, S * i] = XW - 1; h[:, 7, :, S * i] = GW - 1; a[:, 7, :, i] = 0
    g[:, 7, :15, GW - 1] = XW - 1; g[:, 7, 15, GW - 1] = 0
    return pack(g, h, x, a, t)
def setup_inputs_corners(rng):
    g, h, x, a, t = parts(rng); o = rng.permutation(8); t[:, o[0]] = 0; t[:, o[1]] = 4080
    for q in range(N):
        w = rng.permutation(o[2:])
        h[q, w[0]] = np.arange(GW); h[q, w[1]] = (GW - 1) * rng.integers(0, 2, (16, GW)); h[q, w[2]] = np.roll(np.arange(GW), -1)
        g[q, w[3]] = (XW - 1) * rng.integers(0, 2, (16, GW))
        b = w[4]; t[q, b] = 0; x[q, b, :, XW - 1] = 255; g[q, b, 15] = XW - 1
        i = rng.permutation(L)[:L // 2]; a[q, b][:, i] = x[q, b][:, g[q, b, 0, S * i]]
        x[q, w[5]] = 255 * rng.integers(0, 2, (16, XW))
    return pack(g, h, x, a, t)
def setup_inputs_ties(rng):
    g, h, x, a, t = parts(rng)
    x = 8 * rng.integers(0, 32, (N, 8, 1, XW)) + ((np.arange(16)[:, None] == rng.integers(0, 16, (N, 8, 1, XW))) & (rng.random((N, 8, 1, XW)) < 0.5))
    a = 8 * rng.integers(0, 32, (N, 8, 1, L)) + np.zeros((16, 1), np.int64)
    h[:, ::2] = h[:, ::2, :1]
    return pack(g, h, x, a, 16 * (8 * rng.integers(0, 6, (N, 8)) + 1))
def setup_inputs_counts(rng):
    g, h, x, a, t = parts(rng); q = rng.permutation(N); o = rng.permutation(8); w = int(o[0])
    t[q[0]] = 0; t[q[1]] = 4080; t[q[2]] = 4080; t[q[2], o[1:4]] = 0; t[q[3]] = 0
    if N > 4: t[q[4]] = 1170
    if N > 5: t[q[5], o[1:5]] = 0
    t[:, w] = 0; t[q[1], w] = 4080
    u = np.floor(rng.integers(2, 7, (N, 1, XW)) * rng.random((N, 16, XW))).astype(np.int64); u[:, 0] = 0
    x[:, w] = u; x[q[1], w] = 255 - u[q[1]]; x[q[1], w, 0] = 254
    a[:, w] = 255; a[:, w, 0] = 254
    for r, n in ((q[2], 64), (q[3], 8 * int(rng.integers(3, 5)) + int(rng.choice(np.array([2, 3, 5, 6]))))):
        i = rng.permutation(L)[:n]; a[r, w, 0, i] = 255; h[r, w, 0, S * i] = S * i
    return pack(g, h, x, a, t)
def check_inputs(d):
    bad = []
    for k, lo, hi in (("gn", 0, XW - 1), ("nb", 0, GW - 1), ("x", 0, 255), ("th", 0, 4080), ("a0", 0, 255)):
        v = np.asarray(d[k]).astype(np.float64)
        if not (np.min(v) >= lo and np.max(v) <= hi): bad.append("range of " + k)
        elif np.any(v != np.floor(v)): bad.append("whole numbers of " + k)
    v = np.asarray(d["th"]).reshape(-1, 16)
    if np.any(v != v[:, :1]): bad.append("equal rows of th in a group")
    return bad
def reference(gn, nb, x, th, a0):
    G = gn.astype(np.int64).reshape(N, 8, 16, GW); H = nb.astype(np.int64).reshape(N, 8, 16, GW); X = x.astype(np.float32).astype(np.int64).reshape(N, 8, 16, XW)
    lim = th.astype(np.int64).reshape(N, 8, 16)[:, :, :1]; a = a0.astype(np.float32).astype(np.int64).reshape(N, 8, 16, L)
    A = np.zeros(N, np.int64); lane = np.arange(L); kk = np.arange(16)[None, :, None]
    for gen in range(GENS):
        h = np.zeros((N, 8, L), np.int64) + S * lane; p = np.zeros((N, 8, L), np.int64); err = np.zeros((N, 8, L), np.int64)
        dau = G[..., ::S].copy()
        for t in range(ST):
            now = np.zeros(N, np.int64)
            for r in range(N):
                q = (r + t) % N; hr = h[r][:, None, :]; pr = p[r]
                n = np.take_along_axis(np.take_along_axis(G[q], hr, 2), pr[:, None, :], 1)[:, 0]
                T = np.abs(np.take_along_axis(X[q], n[:, None, :], 2) - a[r])
                ho = np.take_along_axis(H[q], hr, 2)
                at = ((pr[:, None, :] + kk) & 15) * GW + ho
                e = np.take_along_axis(G[q].reshape(8, 16 * GW), at.reshape(8, 16 * L), 1)
                v = np.take_along_axis(X[q], e[:, None, :], 2).reshape(8, 16, 16, L)
                D = np.add.reduce(np.abs(v + T[:, :, None, :] - 255), axis=1)
                ok = D <= (lim[q] + (A[q] & 63))[:, :, None]
                found = np.any(ok, axis=1); m = np.argmax(ok, axis=1)
                em = np.take_along_axis(e.reshape(8, 16, L), m[:, None, :], 1)[:, 0]; hm = np.take_along_axis(ho, m[:, None, :], 1)[:, 0]
                an = np.where(found[:, None, :], np.take_along_axis(X[q], em[:, None, :], 2), T)
                dau[r, :, t] = np.where(found, em, n); h[r] = np.where(found, hm, h[r]); p[r] = (pr + 1 + np.where(found, m, 0)) & 15
                err[r] = err[r] + np.where(found, 0, 1); now[q] = np.sum(np.where(found, 0, 1)); a[r] = an
                np.put_along_axis(X[q], (16 * lane + p[r])[:, None, :], an, 2)
            A = now
        order = np.argsort(err * L + lane, axis=2)
        best = np.take_along_axis(dau, order[:, :, None, :K], 3)
        come = np.where((np.arange(K) & 1) == 1, np.roll(best, 1, axis=0), best)
        worst = order[:, :, ::-1][:, :, :K]
        np.put_along_axis(G, (S * worst)[:, :, None, :], come, 3)
    return {"yg": G[..., ::S].reshape(N, 128, L).astype(np.float32), "ya": a.reshape(N, 128, L).astype(np.float32), "ys": np.add.reduce(X.reshape(N, 8, 16, L, 16), axis=4).reshape(N, 128, L).astype(np.float32)}

import numpy as np
from concourse.bass import DstId, RemoteDMATransfer
from concourse.mybir import dt, AluOpType, AxisListType, ActivationFunctionType

OP = AluOpType
AF = ActivationFunctionType
GENS, ST, N = 2, 4, 8
NPOOL = 104

F32, F16, BF, I32, U16 = "float32", "float16", "bfloat16", "int32", "uint16"
SB = {
    "GW": (1184, I32), "NBW": (1152, I32), "XT": (2176, BF), "A0": (128, BF), "TH": (1, I32),
    "PI": (1, I32), "PS": (1, I32), "PL": (1, I32), "PSF": (1, F32), "PLF": (1, F32), "PL1": (1, F32), "F4": (1, F32), "ROWM": (1, F32),
    "MI": (128, I32), "MS": (128, I32), "ML": (128, I32), "ML1": (128, F16), "BLK": (128, F16), "Z": (128, F16),
    "CRF": (2048, F16), "CRB": (2048, BF), "IDB": (128, BF), "F2": (128, F16), "FIRST": (128, F16), "TRI": (128, F32),
    "ALL": (128, F32), "ZER": (128, BF), "DI": (64, I32), "DI2": (64, I32), "DELT": (64, BF), "C16": (8, I32), "ILF": (8, F32),
    "HU0": (16, U16), "NINE": (8, F32), "KC": (8, F32), "B16": (8, I32),
    "HU": (4 * 8, U16), "NBG": (4 * 64, F32), "OFFE": (4 * 64, U16), "D2": (4 * 128, BF), "MASK": (4 * 1024, BF), "GHM": (4 * 64, F16),
    "FBT": (4 * 8, F32), "U1": (4 * 4, F32),
    "NL": (2 * 4, U16), "DD": (2 * 64, BF), "T2": (2 * 128, BF), "TEXP": (2 * 1024, BF), "GG": (2 * 1024, F16), "EL": (2 * 64, U16),
    "UU": (2 * 1024, F32), "AB": (2 * 1024, BF), "OKT": (2 * 64, F16), "PACK": (2 * 320, F16), "NF": (2 * 8, F32), "TMP": (2 * 8, F32),
    "IDXF": (2 * 4, F32), "IDX": (2 * 4, U16), "NFB": (2 * 64, F32), "GHF": (2 * 64, F16),
    "UI": (8, I32), "UI2": (8, I32), "UI3": (8, I32), "POS": (8, U16), "RF": (2, F32), "AI": (1, I32), "AI2": (1, I32), "LIM": (9, F32),
    "DZ": (128, F16), "IND": (128, F16), "NRED": (1, F32), "PRE": (128, F32), "PPK": (128, F16), "POSL": (8, U16), "SD": (128, F32),
    "GEC": (8, F32), "DQ": (8, F32), "MLQ": (8, F32), "IDN": (8, U16), "NEW": (128, F32), "YA": (128, F32), "YS": (128, F32),
    "SA": (16 * 72, F16), "LA": (16 * 72, F16), "SBB": (8 * 256, F16), "LB": (8 * 256, F16), "LE": (4 * 64, F16),
    "SM": (2 * 24, F16), "LM": (2 * 24, F16), "SO": (2 * 16, F16), "LO": (2 * 16, F16),
}
SCRATCH = {}
for _n in SB:
    SCRATCH[_n] = ("sbuf", [128, SB[_n][0]], SB[_n][1])
for _i in range(8):
    SCRATCH["b%d" % _i] = ("psum", [128, 512], F32)


def messages():
    out = []
    for g in range(GENS):
        for t in range(ST):
            s = g * ST + t
            if t < ST - 1:
                for h in range(2):
                    out.append(("ra%d%d%d" % (g, t, h), 1, ("SA", (2 * s + h) * 72, (2 * s + h) * 72 + 72),
                                ("LA", (2 * s + 2 + h) * 72, (2 * s + 2 + h) * 72 + 72), h))
                out.append(("rb%d%d" % (g, t), 1, ("SBB", s * 256, s * 256 + 256), ("LB", (s + 1) * 256, (s + 1) * 256 + 256), 2))
            else:
                for h in range(2):
                    out.append(("re%d%d" % (g, h), N - 3, ("SA", (2 * s + h) * 72, (2 * s + h) * 72 + 64),
                                ("LE", (2 * g + h) * 64, (2 * g + h) * 64 + 64), h))
                out.append(("rm%d" % g, N - 3, ("SM", 24 * g, 24 * g + 24), ("LM", 24 * g, 24 * g + 24), 0))
                out.append(("ro%d" % g, N - 2, ("SO", 16 * g, 16 * g + 16), ("LO", 16 * g, 16 * g + 16), 1))
    return out


MSG = messages()
SEMAPHORES = [m[0] for m in MSG] + ["ls"] + ["dm%d" % i for i in range(8)] + ["p%d" % i for i in range(NPOOL)]


def route(src, dst, topo, pick):
    if topo.may_write(src, dst):
        return [src, dst]
    c = [x for x in topo.cores_of(src) if x != src and topo.may_write(x, dst)]
    c.sort(key=lambda x: (topo.die(x) != topo.die(src), x))
    return [src, c[pick % len(c)], dst]


def hop(g, T, topo, a, b, src, land, sem):
    rid, pid = topo.addr(b, a)
    g.remote_dma(T[land[0]][:, land[1]:land[2]], T[src[0]][:, src[1]:src[2]], T.sem[sem], T.sem["ls"], pid, rid, topo.mask(a, b))
    return len(topo.engines(a, b))


def relay_program(g, core, T, topo):
    owner = [c for c in T.cores if c in topo.cores_of(core)]
    total = 0
    for c in owner:
        r = T.rank_of(c)
        for sem, on, src, land, pick in MSG:
            way = route(c, T.cores[(r + on) % N], topo, pick)
            if len(way) == 3 and way[1] == core:
                g.wait_ge(T.sem[sem], len(topo.engines(c, core)))
                total += hop(g, T, topo, core, way[2], land, land, sem)
    if total:
        g.wait_ge(T.sem["ls"], total)


def bits(lo, hi, step):
    if step == 1:
        return ((1 << (hi - lo)) - 1) << lo
    m = 0
    for i in range(lo, hi, step):
        m |= 1 << i
    return m


class_cache = {}


def new_op(P, q, emit, rd, wr, dur, sem=None, amount=1, sdeps=(), lat=0.0):
    ops, track, banks = P["ops"], P["track"], P["banks"]
    k = len(ops)
    deps = set()
    for acc, isw in [(a, False) for a in rd] + [(a, True) for a in wr]:
        name = acc[0]
        key = (acc[1], acc[2], acc[3] if len(acc) > 3 else 1)
        if key not in class_cache:
            class_cache[key] = bits(*key)
        m = class_cache[key]
        W, R = track.setdefault(name, ([], []))
        for mm, o in W:
            if mm & m and o != k:
                deps.add(o)
        if isw:
            for mm, o in R:
                if mm & m and o != k:
                    deps.add(o)
            W[:] = [(mm & ~m, o) for mm, o in W if mm & ~m] + [(m, k)]
            R[:] = [(mm & ~m, o) for mm, o in R if mm & ~m]
        else:
            R.append((m, k))
        if name in banks:
            for o in banks[name]:
                if o != k and ops[o]["q"] != q:
                    deps.add(o)
            banks[name][:] = [o for o in banks[name] if ops[o]["q"] == q]
            banks[name].append(k)
    banks_fix = None
    ops.append({"q": q, "emit": emit, "deps": deps, "sdeps": set(sdeps), "dur": dur, "sem": sem, "amount": amount, "lat": lat})
    return k


def order_ops(ops):
    n = len(ops)
    wake = 0.06
    prio = [0.0] * n
    succ = [[] for _i in range(n)]
    for k in range(n):
        for d in ops[k]["deps"] | ops[k]["sdeps"]:
            succ[d].append(k)
    for k in range(n - 1, -1, -1):
        o = ops[k]
        prio[k] = o["dur"] + o["lat"] + wake + max([prio[s] for s in succ[k]] or [0.0])
    left = [len(ops[k]["deps"] | ops[k]["sdeps"]) for k in range(n)]
    ready = {}
    free = {}
    cand = {}
    for k in range(n):
        free[ops[k]["q"]] = 0.0
        cand[ops[k]["q"]] = []
    for k in range(n):
        if left[k] == 0:
            cand[ops[k]["q"]].append(k)
            ready[k] = 0.0
    fin = [0.0] * n
    seq = []
    while len(seq) < n:
        best = None
        for q in cand:
            if not cand[q]:
                continue
            if q == "recv":
                k = min(cand[q], key=lambda x: ready[x])
                s = ready[k]
            else:
                s = max(free[q], min([ready[x] for x in cand[q]]))
                k = max([x for x in cand[q] if ready[x] <= s + 1e-9], key=lambda x: (prio[x], -x))
            if best is None or s < best[0]:
                best = (s, k, q)
        s, k, q = best
        cand[q].remove(k)
        if q != "recv":
            free[q] = s + ops[k]["dur"]
        fin[k] = s + ops[k]["dur"] + ops[k]["lat"]
        seq.append(k)
        for c in succ[k]:
            left[c] -= 1
            ready[c] = max(ready.get(c, 0.0), fin[k] + wake)
            if left[c] == 0:
                cand[ops[c]["q"]].append(c)
    return seq, max(fin)


def emit_ops(g, T, ops, seq):
    known, clk, waits, waited = {}, {}, {}, set()
    pos = {k: i for i, k in enumerate(seq)}
    for k in seq:
        o = ops[k]
        if o["q"] == "recv":
            clk[k] = 0
            continue
        kn = known.get(o["q"], 0)
        w = []
        for d in sorted(o["deps"], key=lambda x: -pos[x]):
            if not (kn >> d) & 1:
                w.append(d)
                waited.add(d)
                kn |= (1 << d) | clk[d]
        known[o["q"]] = kn
        clk[k] = kn
        waits[k] = w
    Q = {"V": g.vector, "P": g.tensor, "S": g.scalar, "Y": g.sync, "G": g}
    last, count, at = {}, {}, {}
    pool = ["p%d" % i for i in range(NPOOL)]
    turn = {}
    for k in seq:
        o = ops[k]
        if o["q"] == "recv":
            at[k] = (o["sem"], o["amount"])
            continue
        q = Q[o["q"]]
        for d in waits[k]:
            q.wait_ge(T.sem[at[d][0]], at[d][1])
        ins = o["emit"]()
        if k in waited:
            if o["sem"] is not None:
                at[k] = (o["sem"], o["amount"])
                ins.then_inc(T.sem[o["sem"]], o["amount"])
            else:
                s = None
                for c in pool:
                    if (c not in last) or (clk[k] >> last[c]) & 1:
                        if s is None or turn.get(c, -1) < turn.get(s, -1):
                            s = c
                            if c not in last:
                                break
                count[s] = count.get(s, 0) + 1
                last[s] = k
                turn[s] = pos[k]
                at[k] = (s, count[s])
                ins.then_inc(T.sem[s], 1)
        elif o["sem"] is not None:
            at[k] = (o["sem"], o["amount"])
            ins.then_inc(T.sem[o["sem"]], o["amount"])
            q.wait_ge(T.sem[o["sem"]], o["amount"])


def rank_program(g, core, T, topo):
    rank = T.rank_of(core)
    if rank is None:
        relay_program(g, core, T, topo)
        return
    P = {"ops": [], "track": {}, "banks": {"b%d" % i: [] for i in range(8)}}
    C = 0.00095

    def ap(a):
        if len(a) > 3:
            return T[a[0]][:, a[1]:a[2]:a[3]]
        return T[a[0]][:, a[1]:a[2]]

    def width(a):
        return len(range(a[1], a[2], a[3] if len(a) > 3 else 1))

    def two(*accs):
        return all((a[0] in SB and SB[a[0]][1] in (F16, BF, U16)) for a in accs)

    def vdur(n, f):
        return 0.01 + C * max(64, n * f)

    def cols(*xs):
        return [x for x in xs if isinstance(x, tuple)]

    def val(x):
        return ap(x) if isinstance(x, tuple) else x

    def copy(out, in_):
        new_op(P, "V", lambda: g.vector.tensor_copy(out=ap(out), in_=ap(in_)), [in_], [out], vdur(width(out), 0.5 if two(out, in_) else 1))

    def ts(out, in0, s1, op0, s2=None, op1=None):
        def e():
            if op1 is None:
                return g.vector.tensor_scalar(out=ap(out), in0=ap(in0), scalar1=val(s1), scalar2=None, op0=op0)
            return g.vector.tensor_scalar(out=ap(out), in0=ap(in0), scalar1=val(s1), scalar2=val(s2), op0=op0, op1=op1)
        new_op(P, "V", e, [in0] + cols(s1, s2), [out], vdur(width(out), 0.5 if two(out, in0) else 1))

    def tt(out, in0, in1, op):
        f = 2 if (in0[0] in SB and in1[0] in SB) else 1
        new_op(P, "V", lambda: g.vector.tensor_tensor(out=ap(out), in0=ap(in0), in1=ap(in1), op=op), [in0, in1], [out], vdur(width(out), f))

    def gather(out, win, off):
        new_op(P, "V", lambda: g.vector.tensor_copy(out=ap(out), in_=ap(win).indirect(ap(off))), [win, off], [out], 0.05 + 1.6 * C * width(out))

    def gather2(out, win, off, in1, op):
        new_op(P, "V", lambda: g.vector.tensor_tensor(out=ap(out), in0=ap(win).indirect(ap(off)), in1=ap(in1), op=op), [win, off, in1], [out],
               0.05 + 1.6 * C * width(out))

    def scatter(win, off, in_):
        new_op(P, "V", lambda: g.vector.tensor_copy(out=ap(win).indirect(ap(off)), in_=ap(in_)), [off, in_], [win], 0.05 + 3.5 * C * width(in_))

    def fill(out, c):
        new_op(P, "V", lambda: g.vector.memset(ap(out), c), [], [out], vdur(width(out), 1))

    def act(out, in_, func, accum=None, **kw):
        def e():
            if accum is None:
                return g.scalar.activation(out=ap(out), in_=ap(in_), func=func, **kw)
            return g.scalar.activation(out=ap(out), in_=ap(in_), func=func, accum_out=ap(accum), **kw)
        new_op(P, "S", e, [in_], [out] + cols(accum), 0.05 + C * width(out))

    def mms(out, pairs):
        def e():
            ins = None
            for i, (l, r) in enumerate(pairs):
                ins = g.tensor.matmul(ap(out), ap(l), ap(r), i == 0, i == len(pairs) - 1)
            return ins
        f = 4 if SB[pairs[0][0][0]][1] == F32 else 1
        new_op(P, "P", e, [x for p in pairs for x in p], [out], 0.02 + len(pairs) * C * f * max(64, width(out)))

    def iota(out, pattern, base, cm):
        new_op(P, "G", lambda: g.iota(ap(out), pattern, base, cm), [], [out], 0.13 + 2 * C * width(out))

    def load(q, out, name, sem):
        eng = g.sync if q == "Y" else g.scalar
        new_op(P, q, lambda: eng.dma_start(out=ap(out), in_=T[name][:, :]), [], [out], 0.1, sem=sem, amount=16, lat=3.0)

    def store(name, in_, sem):
        new_op(P, "Y", lambda: g.sync.dma_start(out=T[name][:, :], in_=ap(in_)), [in_], [], 0.1, sem=sem, amount=16, lat=2.0)

    sent = [0]
    by = {m[0]: m for m in MSG}

    def send(sem):
        m = by[sem]
        way = route(core, T.cores[(rank + m[1]) % N], topo, m[4])

        def e():
            sent[0] += hop(g, T, topo, core, way[1], m[2], m[3], sem)
        k = new_op(P, "G", e, [m[2]], [], 1.0)
        back = T.cores[(rank - m[1]) % N]
        cnt = len(topo.engines(route(back, core, topo, m[4])[-2], core))
        new_op(P, "recv", None, [], [m[3]], 0.0, sem=sem, amount=cnt, sdeps=(k,), lat=4.0)

    def sl(name, i, w, lo=0, hi=None, step=1):
        hi = w if hi is None else hi
        if step == 1:
            return (name, i * w + lo, i * w + hi)
        return (name, i * w + lo, i * w + hi, step)

    def C16F(r): return ("CRF", 128 * r, 128 * r + 128)
    def C16B(r): return ("CRB", 128 * r, 128 * r + 128)
    NBWIN, GWIN, XWIN, XALL = ("NBW", 0, 1152), ("GW", 0, 1152), ("XT", 0, 2048), ("XT", 0, 2176)
    full = lambda n: (n, 0, SB[n][0])

    load("Y", NBWIN, "nb", "dm0")
    load("S", GWIN, "gn", "dm1")
    load("Y", full("A0"), "a0", "dm2")
    load("S", full("TH"), "th", "dm3")
    load("Y", XWIN, "x", "dm4")
    iota(full("PI"), [[1, 1]], 0, 1)
    iota(full("MI"), [[1, 128]], 0, 0)
    iota(full("C16"), [[16, 8]], 0, 0)
    iota(full("DI"), [[-1, 64]], 64, 1)
    ts(full("PS"), full("PI"), 4, OP.arith_shift_right)
    ts(full("PL"), full("PI"), 15, OP.bitwise_and)
    copy(full("PSF"), full("PS"))
    copy(full("PLF"), full("PL"))
    ts(full("ILF"), full("C16"), full("PLF"), OP.add)
    fill(full("HU0"), 0)
    for h in range(2):
        ts(("HU0", 8 * h, 8 * h + 4), ("ILF", 4 * h, 4 * h + 4), 9.0, OP.mult)
    ts(full("DI2"), full("DI"), 15, OP.bitwise_and)
    copy(full("DELT"), full("DI2"))
    ts(full("MS"), full("MI"), 4, OP.arith_shift_right)
    ts(full("ML"), full("MI"), 15, OP.bitwise_and)
    ts(full("ML1"), full("ML"), 1.0, OP.add)
    ts(full("BLK"), full("MS"), full("PSF"), OP.is_equal)
    tt(full("Z"), full("ML1"), full("BLK"), OP.mult)
    for r in range(16):
        ts(C16F(r), full("Z"), float(r + 1), OP.is_equal)
    for r in range(16):
        ts(C16B(r), full("Z"), float(r + 1), OP.is_equal)
    ts(full("PL1"), full("PLF"), 1.0, OP.add)
    ts(full("IDB"), full("Z"), full("PL1"), OP.is_equal)
    ts(full("F2"), full("Z"), full("PL1"), OP.is_gt, 2.0, OP.mult)
    tt(full("FIRST"), full("F2"), full("IDB"), OP.add)
    ts(full("TRI"), full("Z"), full("PL1"), OP.is_gt)
    ts(full("F4"), full("PLF"), -1.0, OP.mult, 4.0, OP.add)
    ts(full("ROWM"), full("PLF"), 4.0, OP.is_ge)
    fill(full("ALL"), 0.0625)
    fill(full("ZER"), 0.0)
    ts(full("NINE"), full("ILF"), 9.0, OP.mult)
    ts(full("KC"), full("ILF"), -9.0, OP.mult, 1280.0, OP.add)
    ts(full("B16"), full("ILF"), 16.0, OP.mult)
    for s in range(4):
        h = s & 1
        ts(sl("FBT", s, 8, 0, 4), ("ILF", 4 * h, 4 * h + 4), 2048.0, OP.add)
    copy(("LIM", 0, 1), full("TH"))

    for gen in range(GENS):
        ts(full("DZ"), ("GW", 0, 1152, 9), full("ROWM"), OP.mult)
        for t in range(ST):
            n = gen * ST + t
            end = t == ST - 1
            for h in range(2):
                s4 = 2 * (n & 1) + h
                b = ["b%d" % (4 * h + i) for i in range(4)]
                la = (2 * n + h) * 72
                if t == 0:
                    hl, ul = ("HU0", 8 * h, 8 * h + 4), ("HU0", 8 * h + 4, 8 * h + 8)
                    ts(sl("FBT", s4, 8, 4, 8), ("ILF", 4 * h, 4 * h + 4), 9.0, OP.mult)
                    fill(sl("U1", s4, 4), 1.0)
                    a = ("A0", 64 * h, 64 * h + 64) if gen == 0 else ("LE", 64 * h, 64 * h + 64)
                else:
                    hl, ul = sl("HU", s4, 8, 0, 4), sl("HU", s4, 8, 4, 8)
                    copy(sl("HU", s4, 8), ("LA", la + 64, la + 72))
                    copy(sl("FBT", s4, 8, 4, 8), ("LA", la + 64, la + 68))
                    ts(sl("U1", s4, 4), ("LA", la + 68, la + 72), 1.0, OP.add)
                    a = ("LA", la, la + 64)
                gather(sl("D2", s4, 128, 0, 128, 2), full("DELT"), ul)
                gather(sl("NBG", s4, 64), NBWIN, hl)
                ts(sl("D2", s4, 128, 1, 128, 2), sl("D2", s4, 128, 0, 128, 2), -8.0, OP.add)
                for k in range(8):
                    ts(sl("MASK", s4, 1024, k, 1024, 8), sl("D2", s4, 128), float(k), OP.is_equal)
                gather2(sl("GHM", s4, 64), GWIN, hl, sl("MASK", s4, 1024, 0, 1024, 16), OP.mult)
                copy(sl("OFFE", s4, 64), sl("NBG", s4, 64))
                mms((b[0], 0, 4), [(C16F(r), sl("GHM", s4, 64, r, 64, 16)) for r in range(16)])
                copy(sl("NL", h, 4), (b[0], 0, 4))
                gather2(sl("DD", h, 64), XWIN, sl("NL", h, 4), a, OP.subtract)
                for j in range(2):
                    act(sl("T2", h, 128, j, 128, 2), sl("DD", h, 64), AF.Abs)
                for k in range(8):
                    act(sl("TEXP", h, 1024, k, 1024, 8), sl("T2", h, 128), AF.Copy)
                act(("XT", 2048 + 64 * h, 2112 + 64 * h), sl("DD", h, 64), AF.Abs)
                gather2(sl("GG", h, 1024), GWIN, sl("OFFE", s4, 64), sl("MASK", s4, 1024), OP.mult)
                mms((b[1], 0, 64), [(C16F(k), sl("GG", h, 1024, k, 1024, 16)) for k in range(16)])
                copy(sl("EL", h, 64), (b[1], 0, 64))
                for q in range(2):
                    gather2(sl("UU", h, 1024, 512 * q, 512 * q + 512), XWIN, sl("EL", h, 64, 32 * q, 32 * q + 32),
                            sl("TEXP", h, 1024, 512 * q, 512 * q + 512), OP.add)
                    act(sl("AB", h, 1024, 512 * q, 512 * q + 512), sl("UU", h, 1024, 512 * q, 512 * q + 512), AF.Abs, bias=-255.0)
                mms((b[2], 0, 64), [(C16B(k), sl("AB", h, 1024, k, 1024, 16)) for k in range(16)])
                ts(sl("OKT", h, 64), (b[2], 0, 64), ("LIM", n, n + 1), OP.is_le)
                mms((b[2], 0, 64), [(full("FIRST"), sl("OKT", h, 64))])
                sel = sl("PACK", h, 320, 128, 192)
                ts(sel, (b[2], 0, 64), 1.0, OP.is_equal)
                ts(sl("PACK", h, 320, 192, 256), (b[2], 0, 64), 1.0, OP.is_equal)
                ts(sl("PACK", h, 320, 256, 320), (b[2], 0, 64), 1.0, OP.is_equal, full("PLF"), OP.mult)
                tt(sl("PACK", h, 320, 0, 64), sel, (b[1], 0, 64), OP.mult)
                tt(sl("PACK", h, 320, 64, 128), sel, sl("NBG", s4, 64), OP.mult)
                mms((b[0], 0, 20), [(C16F(r), sl("PACK", h, 320, r, 320, 16)) for r in range(16)])
                ts(sl("NF", h, 8), (b[0], 8, 16), -1.0, OP.mult, 1.0, OP.add)
                tt(sl("TMP", h, 8), sl("NF", h, 8), sl("FBT", s4, 8), OP.mult)
                tt(sl("IDXF", h, 4), sl("TMP", h, 8, 0, 4), (b[0], 0, 4), OP.add)
                copy(sl("IDX", h, 4), sl("IDXF", h, 4))
                sa = (2 * n + h) * 72
                if not end:
                    tt(("SA", sa + 64, sa + 68), sl("TMP", h, 8, 4, 8), (b[0], 4, 8), OP.add)
                tt(("SA", sa + 68, sa + 72), sl("U1", s4, 4), (b[0], 16, 20), OP.add)
                gather(("SA", sa, sa + 64), XALL, sl("IDX", h, 4))
                send("re%d%d" % (gen, h) if end else "ra%d%d%d" % (gen, t, h))
                mms((b[3], 0, 64), [(full("BLK"), sel)])
                act(sl("NFB", h, 64), (b[3], 0, 64), AF.Identity, accum=("RF", h, h + 1), scale=-1.0, bias=1.0)
                fo = ("SBB", 256 * n + 128 + 64 * h, 256 * n + 192 + 64 * h)
                if t == 0:
                    copy(fo, (b[3], 0, 64))
                else:
                    tt(fo, ("LB", 256 * n + 128 + 64 * h, 256 * n + 192 + 64 * h), (b[3], 0, 64), OP.add)
                tt(sl("GHF", h, 64), sl("GHM", s4, 64), sl("NFB", h, 64), OP.mult)
                mms((b[3], 64, 128), [(C16F(t), sl("PACK", h, 320, 0, 64)), (C16F(t), sl("GHF", h, 64))])
                prev = ("DZ", 64 * h, 64 * h + 64) if t == 0 else ("LB", 256 * n + 64 * h, 256 * n + 64 * h + 64)
                tt(("SBB", 256 * n + 64 * h, 256 * n + 64 * h + 64), prev, (b[3], 64, 128), OP.add)
            if not end:
                send("rb%d%d" % (gen, t))
            for h in range(2):
                sa = (2 * n + h) * 72
                copy(("UI", 4 * h, 4 * h + 4), ("SA", sa + 68, sa + 72))
            ts(full("UI2"), full("UI"), 15, OP.bitwise_and)
            tt(full("UI3"), full("UI2"), full("B16"), OP.add)
            copy(full("POS"), full("UI3"))
            for h in range(2):
                sa = (2 * n + h) * 72
                scatter(XWIN, ("POS", 4 * h, 4 * h + 4), ("SA", sa, sa + 64))
            if n < GENS * ST - 1:
                mms(("b3", 128, 129), [(full("ALL"), ("RF", 0, 1)), (full("ALL"), ("RF", 1, 2))])
                copy(full("AI"), ("b3", 128, 129))
                ts(full("AI2"), full("AI"), 63, OP.bitwise_and)
                tt(("LIM", n + 1, n + 2), full("AI2"), full("TH"), OP.add)
        n = gen * ST + ST - 1
        ts(full("IND"), ("SBB", 256 * n + 128, 256 * n + 256), full("F4"), OP.is_equal)
        new_op(P, "V", lambda: g.vector.tensor_reduce(out=ap(full("NRED")), in_=ap(full("IND")), axis=AxisListType.X, op=OP.add),
               [full("IND")], [full("NRED")], 0.15)
        mms(("b0", 32, 33), [(full("TRI"), full("NRED"))])
        new_op(P, "V", lambda: g.vector.tensor_tensor_scan(out=ap(full("PRE")), data0=ap(full("ZER")), data1=ap(full("IND")),
                                                           initial=ap(("b0", 32, 33)), op0=OP.add, op1=OP.add),
               [full("IND"), full("ZER"), ("b0", 32, 33)], [full("PRE")], 0.15)
        tt(full("PPK"), full("PRE"), full("IND"), OP.mult)
        mms(("b4", 0, 8), [(C16F(r), ("PPK", r, 128, 16)) for r in range(16)])
        ts(full("POSL"), ("b4", 0, 8), -1.0, OP.add)
        scatter(full("SD"), full("POSL"), ("SBB", 256 * n, 256 * n + 128))
        copy(("SM", 24 * gen + 8, 24 * gen + 24), ("SD", 0, 32, 2))
        copy(("SO", 16 * gen, 16 * gen + 16), ("SD", 1, 32, 2))
        ts(full("GEC"), ("b4", 0, 8), 97.0, OP.is_ge)
        tt(full("DQ"), full("KC"), ("b4", 0, 8), OP.subtract)
        tt(full("MLQ"), full("GEC"), full("DQ"), OP.mult)
        tt(("SM", 24 * gen, 24 * gen + 8), full("MLQ"), full("NINE"), OP.add)
        send("rm%d" % gen)
        send("ro%d" % gen)
        copy(full("IDN"), ("LM", 24 * gen, 24 * gen + 8))
        copy(("GW", 1152, 1184, 2), ("LM", 24 * gen + 8, 24 * gen + 24))
        copy(("GW", 1153, 1184, 2), ("LO", 16 * gen, 16 * gen + 16))
        gather(full("NEW"), ("GW", 0, 1184), full("IDN"))
        if gen < GENS - 1:
            copy(("GW", 0, 1152, 9), full("NEW"))
    store("yg", full("NEW"), "dm5")
    for h in range(2):
        copy(("YA", 64 * h, 64 * h + 64), ("LE", 128 + 64 * h, 192 + 64 * h))
    store("ya", full("YA"), "dm6")
    mms(("b7", 0, 128), [(full("IDB"), ("XT", j, 2048, 16)) for j in range(16)])
    copy(full("YS"), ("b7", 0, 128))
    store("ys", full("YS"), "dm7")

    seq, total = order_ops(P["ops"])
    emit_ops(g, T, P["ops"], seq)
    g.wait_ge(T.sem["ls"], sent[0])
